import numpy as np
CORES = [16,20,17,21,18,22,19,23,24,28,25,29,26,30,27,31]
N = 16
def setup_inputs(rng):
    return {"x": rng.standard_normal((N, 128, 1024), dtype=np.float32)}
def reference(x):
    g = np.concatenate(list(x), axis=1)
    return {"y": np.broadcast_to(g, (N,) + g.shape)}

@@ -1,0 +1,71 @@
+import concourse.bass as bass
+
+C = 1
+W = 1024 // C
+SCRATCH = {
+    "land": ("sbuf", [128, 16384], "float32"),
+}
+SEMAPHORES = (["ld%d" % i for i in range(8)] + ["on%d" % i for i in range(8)] + ["xa%d" % i for i in range(8)]
+              + ["fw%d" % i for i in range(8)] + ["st", "sent"])
+
+RELAY_SRC = {2: 0, 3: 1, 6: 4, 7: 5}
+
+
+def rank_program(g, core, T, topo):
+    s = T.sem
+    ld = [s.ld0, s.ld1, s.ld2, s.ld3, s.ld4, s.ld5, s.ld6, s.ld7]
+    on = [s.on0, s.on1, s.on2, s.on3, s.on4, s.on5, s.on6, s.on7]
+    xa = [s.xa0, s.xa1, s.xa2, s.xa3, s.xa4, s.xa5, s.xa6, s.xa7]
+    fw = [s.fw0, s.fw1, s.fw2, s.fw3, s.fw4, s.fw5, s.fw6, s.fw7]
+    ch, k = topo.chip(core), core % 8
+    rank = T.rank_of(core)
+
+    def blk(r, c):
+        return T.land[:, r * 1024 + c * W: r * 1024 + (c + 1) * W]
+
+    def send(dst, ap, sem):
+        a = topo.addr(dst)
+        g.remote_dma(ap, ap, remote_sem=sem, local_sem=s.sent, pid=a[1], routing_id=a[0], dma_engine_mask=0x00FF)
+
+    def fan(dsts, ap, sem):
+        ids = [bass.DstId(rid=topo.addr(d)[0], pnc=topo.addr(d)[1]) for d in dsts]
+        g.remote_dma_fused([bass.RemoteDMATransfer(dst_ids=ids, dma_engine_mask=0xFFFF, remote_sem=sem,
+                                                   srcs=[ap], dsts=[ap] * len(dsts))], local_sem=s.sent)
+
+    if rank is None:
+        if k in RELAY_SRC:
+            src = (ch + 2) * 8 + RELAY_SRC[k]
+            dst = ((ch + 2) ^ 1) * 8 + RELAY_SRC[k]
+            r = T.rank_of(src)
+            for c in range(C):
+                g.wait_ge(xa[c], 8)
+                send(dst, blk(r, c), xa[c])
+            g.wait_ge(s.sent, 8 * C)
+        return
+
+    peers = [ch * 8 + i for i in range(8) if i != k]
+    twin = (ch ^ 1) * 8 + k
+    rx = T.rank_of(twin)
+    own_half = min(T.rank_of(p) for p in peers + [core]) * 1024
+    far_half = 8192 - own_half
+
+    for c in range(C):
+        g.dma_start(blk(rank, c), T.x[:, c * W:(c + 1) * W]).then_inc(ld[c], 16)
+    for c in range(C):
+        g.wait_ge(ld[c], 16)
+        if topo.may_write(core, twin):
+            send(twin, blk(rank, c), xa[c])
+        else:
+            send((ch - 2) * 8 + k + 2, blk(rank, c), xa[c])
+        fan(peers, blk(rank, c), on[c])
+    for c in range(C):
+        g.wait_ge(xa[c], 8)
+        fan(peers, blk(rx, c), fw[c])
+    for c in range(C):
+        g.wait_ge(on[c], 7 * 16)
+    g.dma_start(T.y[:, own_half:own_half + 8192], T.land[:, own_half:own_half + 8192]).then_inc(s.st, 16)
+    for c in range(C):
+        g.wait_ge(fw[c], 7 * 16)
+    g.dma_start(T.y[:, far_half:far_half + 8192], T.land[:, far_half:far_half + 8192]).then_inc(s.st, 16)
+    g.wait_ge(s.st, 32)
+    g.wait_ge(s.sent, 40 * C)

@@ -6,7 +6,7 @@ SCRATCH = {
     "land": ("sbuf", [128, 16384], "float32"),
 }
 SEMAPHORES = (["ld%d" % i for i in range(8)] + ["on%d" % i for i in range(8)] + ["xa%d" % i for i in range(8)]
-              + ["fw%d" % i for i in range(8)] + ["st", "sent"])
+              + ["fw%d" % i for i in range(8)] + ["fr%d" % i for i in range(8)] + ["st", "sent"])
 
 RELAY_SRC = {2: 0, 3: 1, 6: 4, 7: 5}
 
@@ -17,6 +17,7 @@ def rank_program(g, core, T, topo):
     on = [s.on0, s.on1, s.on2, s.on3, s.on4, s.on5, s.on6, s.on7]
     xa = [s.xa0, s.xa1, s.xa2, s.xa3, s.xa4, s.xa5, s.xa6, s.xa7]
     fw = [s.fw0, s.fw1, s.fw2, s.fw3, s.fw4, s.fw5, s.fw6, s.fw7]
+    fr = [s.fr0, s.fr1, s.fr2, s.fr3, s.fr4, s.fr5, s.fr6, s.fr7]
     ch, k = topo.chip(core), core % 8
     rank = T.rank_of(core)
 
@@ -48,24 +49,31 @@ def rank_program(g, core, T, topo):
     rx = T.rank_of(twin)
     own_half = min(T.rank_of(p) for p in peers + [core]) * 1024
     far_half = 8192 - own_half
+    direct = topo.may_write(core, twin)
+
+    def store(col, n):
+        g.dma_start(T.y[:, col:col + n], T.land[:, col:col + n]).then_inc(s.st, 16)
 
     for c in range(C):
         g.dma_start(blk(rank, c), T.x[:, c * W:(c + 1) * W]).then_inc(ld[c], 16)
     for c in range(C):
         g.wait_ge(ld[c], 16)
-        if topo.may_write(core, twin):
+        if direct:
             send(twin, blk(rank, c), xa[c])
         else:
             send((ch - 2) * 8 + k + 2, blk(rank, c), xa[c])
         fan(peers, blk(rank, c), on[c])
     for c in range(C):
         g.wait_ge(xa[c], 8)
-        fan(peers, blk(rx, c), fw[c])
+        fan(peers, blk(rx, c), (fw if direct else fr)[c])
     for c in range(C):
         g.wait_ge(on[c], 7 * 16)
-    g.dma_start(T.y[:, own_half:own_half + 8192], T.land[:, own_half:own_half + 8192]).then_inc(s.st, 16)
+    store(own_half, 8192)
     for c in range(C):
-        g.wait_ge(fw[c], 7 * 16)
-    g.dma_start(T.y[:, far_half:far_half + 8192], T.land[:, far_half:far_half + 8192]).then_inc(s.st, 16)
-    g.wait_ge(s.st, 32)
+        g.wait_ge(fw[c], (3 if direct else 4) * 16)
+    store(far_half + 4096, 4096)
+    for c in range(C):
+        g.wait_ge(fr[c], (4 if direct else 3) * 16)
+    store(far_half, 4096)
+    g.wait_ge(s.st, 48)
     g.wait_ge(s.sent, 40 * C)

@@ -1,28 +1,20 @@
 import concourse.bass as bass
 
-C = 1
-W = 1024 // C
 SCRATCH = {
     "land": ("sbuf", [128, 16384], "float32"),
 }
-SEMAPHORES = (["ld%d" % i for i in range(8)] + ["on%d" % i for i in range(8)] + ["xa%d" % i for i in range(8)]
-              + ["fw%d" % i for i in range(8)] + ["fr%d" % i for i in range(8)] + ["st", "sent"])
+SEMAPHORES = ["ld", "st", "sent", "xa", "pa", "pb", "on", "fw", "fr"]
 
 RELAY_SRC = {2: 0, 3: 1, 6: 4, 7: 5}
 
 
 def rank_program(g, core, T, topo):
     s = T.sem
-    ld = [s.ld0, s.ld1, s.ld2, s.ld3, s.ld4, s.ld5, s.ld6, s.ld7]
-    on = [s.on0, s.on1, s.on2, s.on3, s.on4, s.on5, s.on6, s.on7]
-    xa = [s.xa0, s.xa1, s.xa2, s.xa3, s.xa4, s.xa5, s.xa6, s.xa7]
-    fw = [s.fw0, s.fw1, s.fw2, s.fw3, s.fw4, s.fw5, s.fw6, s.fw7]
-    fr = [s.fr0, s.fr1, s.fr2, s.fr3, s.fr4, s.fr5, s.fr6, s.fr7]
     ch, k = topo.chip(core), core % 8
     rank = T.rank_of(core)
 
-    def blk(r, c):
-        return T.land[:, r * 1024 + c * W: r * 1024 + (c + 1) * W]
+    def blk(r):
+        return T.land[:, r * 1024: (r + 1) * 1024]
 
     def send(dst, ap, sem):
         a = topo.addr(dst)
@@ -37,43 +29,39 @@ def rank_program(g, core, T, topo):
         if k in RELAY_SRC:
             src = (ch + 2) * 8 + RELAY_SRC[k]
             dst = ((ch + 2) ^ 1) * 8 + RELAY_SRC[k]
-            r = T.rank_of(src)
-            for c in range(C):
-                g.wait_ge(xa[c], 8)
-                send(dst, blk(r, c), xa[c])
-            g.wait_ge(s.sent, 8 * C)
+            g.wait_ge(s.xa, 8)
+            send(dst, blk(T.rank_of(src)), s.xa)
+            g.wait_ge(s.sent, 8)
         return
 
-    peers = [ch * 8 + i for i in range(8) if i != k]
+    mates = [ch * 8 + i for i in range(8) if i != k and i // 4 == k // 4]
+    partner = ch * 8 + (k ^ 4)
     twin = (ch ^ 1) * 8 + k
-    rx = T.rank_of(twin)
-    own_half = min(T.rank_of(p) for p in peers + [core]) * 1024
+    own_half = (rank // 8) * 8192
     far_half = 8192 - own_half
     direct = topo.may_write(core, twin)
+    far_sem = s.fw if direct else s.fr
 
     def store(col, n):
         g.dma_start(T.y[:, col:col + n], T.land[:, col:col + n]).then_inc(s.st, 16)
 
-    for c in range(C):
-        g.dma_start(blk(rank, c), T.x[:, c * W:(c + 1) * W]).then_inc(ld[c], 16)
-    for c in range(C):
-        g.wait_ge(ld[c], 16)
-        if direct:
-            send(twin, blk(rank, c), xa[c])
-        else:
-            send((ch - 2) * 8 + k + 2, blk(rank, c), xa[c])
-        fan(peers, blk(rank, c), on[c])
-    for c in range(C):
-        g.wait_ge(xa[c], 8)
-        fan(peers, blk(rx, c), (fw if direct else fr)[c])
-    for c in range(C):
-        g.wait_ge(on[c], 7 * 16)
+    g.dma_start(blk(rank), T.x[:, :]).then_inc(s.ld, 16)
+    g.wait_ge(s.ld, 16)
+    send(twin if direct else (ch - 2) * 8 + k + 2, blk(rank), s.xa)
+    fan([partner], blk(rank), s.pa)
+    fan(mates, blk(rank), s.on)
+    g.wait_ge(s.pa, 16)
+    fan(mates, blk(T.rank_of(partner)), s.on)
+    g.wait_ge(s.xa, 8)
+    fan([partner], blk(T.rank_of(twin)), s.pb)
+    fan(mates, blk(T.rank_of(twin)), far_sem)
+    g.wait_ge(s.pb, 16)
+    fan(mates, blk(T.rank_of(twin ^ 4)), far_sem)
+    g.wait_ge(s.on, 6 * 16)
     store(own_half, 8192)
-    for c in range(C):
-        g.wait_ge(fw[c], (3 if direct else 4) * 16)
+    g.wait_ge(s.fw, (2 if direct else 4) * 16)
     store(far_half + 4096, 4096)
-    for c in range(C):
-        g.wait_ge(fr[c], (4 if direct else 3) * 16)
+    g.wait_ge(s.fr, (4 if direct else 2) * 16)
     store(far_half, 4096)
     g.wait_ge(s.st, 48)
-    g.wait_ge(s.sent, 40 * C)
+    g.wait_ge(s.sent, 8 + 6 * 16)

@@ -34,7 +34,7 @@ def rank_program(g, core, T, topo):
             g.wait_ge(s.sent, 8)
         return
 
-    mates = [ch * 8 + i for i in range(8) if i != k and i // 4 == k // 4]
+    mates = [ch * 8 + (k // 4) * 4 + (k + i) % 4 for i in (1, 2, 3)]
     partner = ch * 8 + (k ^ 4)
     twin = (ch ^ 1) * 8 + k
     own_half = (rank // 8) * 8192

@@ -3,7 +3,7 @@ import concourse.bass as bass
 SCRATCH = {
     "land": ("sbuf", [128, 16384], "float32"),
 }
-SEMAPHORES = ["ld", "st", "sent", "xa", "pa", "pb", "on", "fw", "fr"]
+SEMAPHORES = ["ld", "st", "sent", "xa", "pa", "pb", "on", "f0", "f1", "f2", "f3"]
 
 RELAY_SRC = {2: 0, 3: 1, 6: 4, 7: 5}
 
@@ -40,28 +40,33 @@ def rank_program(g, core, T, topo):
     own_half = (rank // 8) * 8192
     far_half = 8192 - own_half
     direct = topo.may_write(core, twin)
-    far_sem = s.fw if direct else s.fr
+    way_out = twin if direct else (ch - 2) * 8 + k + 2
+    late = k % 2 == 1
+    fs = [s.f0, s.f1, s.f2, s.f3]
 
     def store(col, n):
         g.dma_start(T.y[:, col:col + n], T.land[:, col:col + n]).then_inc(s.st, 16)
 
     g.dma_start(blk(rank), T.x[:, :]).then_inc(s.ld, 16)
     g.wait_ge(s.ld, 16)
-    send(twin if direct else (ch - 2) * 8 + k + 2, blk(rank), s.xa)
+    if not late:
+        send(way_out, blk(rank), s.xa)
     fan([partner], blk(rank), s.pa)
     fan(mates, blk(rank), s.on)
+    if late:
+        send(way_out, blk(rank), s.xa)
     g.wait_ge(s.pa, 16)
     fan(mates, blk(T.rank_of(partner)), s.on)
     g.wait_ge(s.xa, 8)
     fan([partner], blk(T.rank_of(twin)), s.pb)
-    fan(mates, blk(T.rank_of(twin)), far_sem)
+    fan(mates, blk(T.rank_of(twin)), fs[k % 4])
     g.wait_ge(s.pb, 16)
-    fan(mates, blk(T.rank_of(twin ^ 4)), far_sem)
+    fan(mates, blk(T.rank_of(twin ^ 4)), fs[k % 4])
     g.wait_ge(s.on, 6 * 16)
     store(own_half, 8192)
-    g.wait_ge(s.fw, (2 if direct else 4) * 16)
-    store(far_half + 4096, 4096)
-    g.wait_ge(s.fr, (4 if direct else 2) * 16)
-    store(far_half, 4096)
-    g.wait_ge(s.st, 48)
+    for j in (2, 3, 0, 1):
+        if j != k % 4:
+            g.wait_ge(fs[j], 2 * 16)
+        store(far_half + j * 2048, 2048)
+    g.wait_ge(s.st, 5 * 16)
     g.wait_ge(s.sent, 8 + 6 * 16)

@@ -3,7 +3,7 @@ import concourse.bass as bass
 SCRATCH = {
     "land": ("sbuf", [128, 16384], "float32"),
 }
-SEMAPHORES = ["ld", "st", "sent", "xa", "pa", "pb", "on", "f0", "f1", "f2", "f3"]
+SEMAPHORES = ["ld", "st", "sent", "xa", "xb", "pa", "pb", "on", "f0", "f1", "f2", "f3"]
 
 RELAY_SRC = {2: 0, 3: 1, 6: 4, 7: 5}
 
@@ -16,6 +16,9 @@ def rank_program(g, core, T, topo):
     def blk(r):
         return T.land[:, r * 1024: (r + 1) * 1024]
 
+    def half(r, h):
+        return T.land[:, r * 1024 + h * 512: r * 1024 + (h + 1) * 512]
+
     def send(dst, ap, sem):
         a = topo.addr(dst)
         g.remote_dma(ap, ap, remote_sem=sem, local_sem=s.sent, pid=a[1], routing_id=a[0], dma_engine_mask=0x00FF)
@@ -27,11 +30,13 @@ def rank_program(g, core, T, topo):
 
     if rank is None:
         if k in RELAY_SRC:
-            src = (ch + 2) * 8 + RELAY_SRC[k]
+            r = T.rank_of((ch + 2) * 8 + RELAY_SRC[k])
             dst = ((ch + 2) ^ 1) * 8 + RELAY_SRC[k]
             g.wait_ge(s.xa, 8)
-            send(dst, blk(T.rank_of(src)), s.xa)
-            g.wait_ge(s.sent, 8)
+            send(dst, half(r, 0), s.xa)
+            g.wait_ge(s.xb, 8)
+            send(dst, half(r, 1), s.xb)
+            g.wait_ge(s.sent, 16)
         return
 
     mates = [ch * 8 + (k // 4) * 4 + (k + i) % 4 for i in (1, 2, 3)]
@@ -40,33 +45,47 @@ def rank_program(g, core, T, topo):
     own_half = (rank // 8) * 8192
     far_half = 8192 - own_half
     direct = topo.may_write(core, twin)
-    way_out = twin if direct else (ch - 2) * 8 + k + 2
     late = k % 2 == 1
     fs = [s.f0, s.f1, s.f2, s.f3]
 
     def store(col, n):
         g.dma_start(T.y[:, col:col + n], T.land[:, col:col + n]).then_inc(s.st, 16)
 
+    def cross():
+        if direct:
+            send(twin, blk(rank), s.xa)
+        else:
+            send((ch - 2) * 8 + k + 2, half(rank, 0), s.xa)
+            send((ch - 2) * 8 + k + 2, half(rank, 1), s.xb)
+
+    def store_own_half():
+        g.wait_ge(s.on, 6 * 16)
+        store(own_half, 8192)
+
     g.dma_start(blk(rank), T.x[:, :]).then_inc(s.ld, 16)
     g.wait_ge(s.ld, 16)
     if not late:
-        send(way_out, blk(rank), s.xa)
+        cross()
     fan([partner], blk(rank), s.pa)
     fan(mates, blk(rank), s.on)
     if late:
-        send(way_out, blk(rank), s.xa)
+        cross()
     g.wait_ge(s.pa, 16)
     fan(mates, blk(T.rank_of(partner)), s.on)
+    if late and not direct:
+        store_own_half()
     g.wait_ge(s.xa, 8)
+    if not direct:
+        g.wait_ge(s.xb, 8)
     fan([partner], blk(T.rank_of(twin)), s.pb)
     fan(mates, blk(T.rank_of(twin)), fs[k % 4])
     g.wait_ge(s.pb, 16)
     fan(mates, blk(T.rank_of(twin ^ 4)), fs[k % 4])
-    g.wait_ge(s.on, 6 * 16)
-    store(own_half, 8192)
+    if direct or not late:
+        store_own_half()
     for j in (2, 3, 0, 1):
         if j != k % 4:
             g.wait_ge(fs[j], 2 * 16)
         store(far_half + j * 2048, 2048)
     g.wait_ge(s.st, 5 * 16)
-    g.wait_ge(s.sent, 8 + 6 * 16)
+    g.wait_ge(s.sent, (8 if direct else 16) + 6 * 16)

@@ -47,9 +47,11 @@ def rank_program(g, core, T, topo):
     direct = topo.may_write(core, twin)
     late = k % 2 == 1
     fs = [s.f0, s.f1, s.f2, s.f3]
+    stores = []
 
     def store(col, n):
         g.dma_start(T.y[:, col:col + n], T.land[:, col:col + n]).then_inc(s.st, 16)
+        stores.append(col)
 
     def cross():
         if direct:
@@ -58,11 +60,20 @@ def rank_program(g, core, T, topo):
             send((ch - 2) * 8 + k + 2, half(rank, 0), s.xa)
             send((ch - 2) * 8 + k + 2, half(rank, 1), s.xb)
 
-    def store_own_half():
+    def store_own_rest(done):
         g.wait_ge(s.on, 6 * 16)
-        store(own_half, 8192)
+        b = 0
+        while b < 8:
+            e = b
+            while e < 8 and e not in done:
+                e += 1
+            if e > b:
+                store(own_half + b * 1024, (e - b) * 1024)
+            b = e + 1
 
     g.dma_start(blk(rank), T.x[:, :]).then_inc(s.ld, 16)
+    g.dma_start(T.y[:, rank * 1024:(rank + 1) * 1024], T.x[:, :]).then_inc(s.st, 16)
+    stores.append(rank * 1024)
     g.wait_ge(s.ld, 16)
     if not late:
         cross()
@@ -73,7 +84,8 @@ def rank_program(g, core, T, topo):
     g.wait_ge(s.pa, 16)
     fan(mates, blk(T.rank_of(partner)), s.on)
     if late and not direct:
-        store_own_half()
+        store(T.rank_of(partner) * 1024, 1024)
+        store_own_rest([rank % 8, T.rank_of(partner) % 8])
     g.wait_ge(s.xa, 8)
     if not direct:
         g.wait_ge(s.xb, 8)
@@ -82,10 +94,10 @@ def rank_program(g, core, T, topo):
     g.wait_ge(s.pb, 16)
     fan(mates, blk(T.rank_of(twin ^ 4)), fs[k % 4])
     if direct or not late:
-        store_own_half()
+        store_own_rest([rank % 8])
     for j in (2, 3, 0, 1):
         if j != k % 4:
             g.wait_ge(fs[j], 2 * 16)
         store(far_half + j * 2048, 2048)
-    g.wait_ge(s.st, 5 * 16)
+    g.wait_ge(s.st, 16 * len(stores))
     g.wait_ge(s.sent, (8 if direct else 16) + 6 * 16)

import concourse.bass as bass

SCRATCH = {
    "land": ("sbuf", [128, 16384], "float32"),
}
SEMAPHORES = ["ld", "st", "sent", "xa", "xb", "pa", "pb", "on", "f0", "f1", "f2", "f3"]

RELAY_SRC = {2: 0, 3: 1, 6: 4, 7: 5}


def rank_program(g, core, T, topo):
    s = T.sem
    ch, k = topo.chip(core), core % 8
    rank = T.rank_of(core)

    def blk(r):
        return T.land[:, r * 1024: (r + 1) * 1024]

    def half(r, h):
        return T.land[:, r * 1024 + h * 512: r * 1024 + (h + 1) * 512]

    def send(dst, ap, sem):
        a = topo.addr(dst)
        g.remote_dma(ap, ap, remote_sem=sem, local_sem=s.sent, pid=a[1], routing_id=a[0], dma_engine_mask=0x00FF)

    def fan(dsts, ap, sem):
        ids = [bass.DstId(rid=topo.addr(d)[0], pnc=topo.addr(d)[1]) for d in dsts]
        g.remote_dma_fused([bass.RemoteDMATransfer(dst_ids=ids, dma_engine_mask=0xFFFF, remote_sem=sem,
                                                   srcs=[ap], dsts=[ap] * len(dsts))], local_sem=s.sent)

    if rank is None:
        if k in RELAY_SRC:
            r = T.rank_of((ch + 2) * 8 + RELAY_SRC[k])
            dst = ((ch + 2) ^ 1) * 8 + RELAY_SRC[k]
            g.wait_ge(s.xa, 8)
            send(dst, half(r, 0), s.xa)
            g.wait_ge(s.xb, 8)
            send(dst, half(r, 1), s.xb)
            g.wait_ge(s.sent, 16)
        return

    mates = [ch * 8 + (k // 4) * 4 + (k + i) % 4 for i in (1, 2, 3)]
    partner = ch * 8 + (k ^ 4)
    twin = (ch ^ 1) * 8 + k
    own_half = (rank // 8) * 8192
    far_half = 8192 - own_half
    direct = topo.may_write(core, twin)
    late = k % 2 == 1
    fs = [s.f0, s.f1, s.f2, s.f3]
    stores = []

    def store(col, n):
        g.dma_start(T.y[:, col:col + n], T.land[:, col:col + n]).then_inc(s.st, 16)
        stores.append(col)

    def cross():
        if direct:
            send(twin, blk(rank), s.xa)
        else:
            send((ch - 2) * 8 + k + 2, half(rank, 0), s.xa)
            send((ch - 2) * 8 + k + 2, half(rank, 1), s.xb)

    def store_own_rest(done):
        g.wait_ge(s.on, 6 * 16)
        b = 0
        while b < 8:
            e = b
            while e < 8 and e not in done:
                e += 1
            if e > b:
                store(own_half + b * 1024, (e - b) * 1024)
            b = e + 1

    g.dma_start(blk(rank), T.x[:, :]).then_inc(s.ld, 16)
    g.dma_start(T.y[:, rank * 1024:(rank + 1) * 1024], T.x[:, :]).then_inc(s.st, 16)
    stores.append(rank * 1024)
    g.wait_ge(s.ld, 16)
    if not late:
        cross()
    fan([partner], blk(rank), s.pa)
    fan(mates, blk(rank), s.on)
    if late:
        cross()
    g.wait_ge(s.pa, 16)
    fan(mates, blk(T.rank_of(partner)), s.on)
    if late and not direct:
        store(T.rank_of(partner) * 1024, 1024)
        store_own_rest([rank % 8, T.rank_of(partner) % 8])
    g.wait_ge(s.xa, 8)
    if not direct:
        g.wait_ge(s.xb, 8)
    fan([partner], blk(T.rank_of(twin)), s.pb)
    fan(mates, blk(T.rank_of(twin)), fs[k % 4])
    g.wait_ge(s.pb, 16)
    fan(mates, blk(T.rank_of(twin ^ 4)), fs[k % 4])
    if direct or not late:
        store_own_rest([rank % 8])
    for j in (2, 3, 0, 1):
        if j != k % 4:
            g.wait_ge(fs[j], 2 * 16)
        store(far_half + j * 2048, 2048)
    g.wait_ge(s.st, 16 * len(stores))
    g.wait_ge(s.sent, (8 if direct else 16) + 6 * 16)
